import numpy as np
import ml_dtypes


def mxq(x, axis, fmt="e4m3"):
    dtype, down = {"e4m3": (ml_dtypes.float8_e4m3fn, 7), "e5m2": (ml_dtypes.float8_e5m2, 14)}[fmt]
    v = np.moveaxis(np.asarray(x, np.float32).astype(ml_dtypes.bfloat16).astype(np.float64), axis, -1)
    blocks = v.reshape(v.shape[:-1] + (-1, 32))
    amax = np.abs(blocks).max(-1, keepdims=True)
    byte = np.maximum(np.where(amax > 0, np.frexp(amax)[1] - 1 + 127, 0) - down, 1)
    scale = np.exp2(byte - 127.0)
    codes = (blocks / scale).astype(np.float32).astype(dtype).astype(np.float64)
    return np.moveaxis((codes * scale).reshape(v.shape), -1, axis)


WIDE = False


def mx_kscale(k):
    if not WIDE:
        return np.ones(k)
    levels = np.array([10, -10, 5, -5, 0])
    if k % 512:
        return np.exp2(np.random.permutation(np.resize(levels, k // 32))).repeat(32)
    a = np.empty((k // 512, 16))
    for p in range(k // 512):
        a[p, :8] = np.random.permutation(np.resize(levels, 8))
        for g in range(8):
            far = levels[np.abs(levels - a[p, g]) >= 10]
            a[p, g + 8] = far[np.random.randint(len(far))]
    return np.exp2(a.ravel()).repeat(32)


def f64(x):
    return np.asarray(x).astype(np.float64)


def striped(idx):
    return np.tile(idx.reshape(-1, 16).T, (8, 1)).astype(np.uint16)


def unstriped(offs):
    return offs[:16].T.reshape(-1).astype(np.int64)


E2M1 = np.array([0.0, 0.5, 1.0, 1.5, 2.0, 3.0, 4.0, 6.0, -0.0, -0.5, -1.0, -1.5, -2.0, -3.0, -4.0, -6.0])


def pack_weight(w, fmt):
    k, n = w.shape
    w = f64(np.asarray(w, np.float32).astype(ml_dtypes.bfloat16)).reshape(k // 32, 32, n)
    amax = np.abs(w).max(1)
    if fmt == "e4m3":
        byte = np.frexp(amax)[1] - 1 + 127 - 7
    else:
        mant, ex = np.frexp(amax / 6.0)
        byte = np.where(mant > 0.5, ex, ex - 1) + 127
    byte = np.clip(np.where(amax > 0, byte, 1), 1, 254)
    scaled = (w * np.exp2(127.0 - byte)[:, None, :]).reshape(k, n).astype(np.float32)
    by_word = np.ascontiguousarray(scaled.reshape(k // 512, 128, 4, n).transpose(0, 1, 3, 2))
    if fmt == "e4m3":
        words = by_word.astype(ml_dtypes.float8_e4m3fn).view(np.uint8)
    else:
        c = by_word.astype(ml_dtypes.float4_e2m1fn).view(np.uint8) & 0xF
        words = (c[..., 0::2] | (c[..., 1::2] << 4)).reshape(k // 512, 128, 2 * n)
    return np.ascontiguousarray(words), np.ascontiguousarray(byte.astype(np.uint8).reshape(k // 512, 16, n))


def unpack_weight(words, scales, fmt):
    g, _, n = scales.shape
    words = np.ascontiguousarray(words).reshape(g, 128, n, -1)
    if fmt == "e4m3":
        vals = words.view(ml_dtypes.float8_e4m3fn).astype(np.float64)
    else:
        nib = np.empty((g, 128, n, 4), np.uint8)
        nib[..., 0::2] = words & 0xF
        nib[..., 1::2] = words >> 4
        vals = E2M1[nib]
    vals = vals * np.repeat(np.exp2(scales.astype(np.float64) - 127.0), 8, axis=1)[..., None]
    return vals.transpose(0, 1, 3, 2).reshape(g * 512, n)


def pack_table(v):
    words, scales = pack_weight(v, "e4m3")
    return np.concatenate([words.reshape(words.shape[0], -1), scales.reshape(scales.shape[0], -1)], axis=1)


def unpack_table(tab):
    g, t = tab.shape[0], tab.shape[1] // 528
    return unpack_weight(tab[:, :512 * t].reshape(g, 128, t, 4), tab[:, 512 * t:].reshape(g, 16, t), "e4m3")


K, L, M, T, S = 1536, 1536, 256, 512, 256


def setup_inputs():
    n = np.random.standard_normal
    s1 = mx_kscale(K)[:, None]
    s2 = mx_kscale(L)[:, None]
    p_w4 = pack_weight(n((K, M)) / np.sqrt(K) / s1, "e2m1")
    return {
        "tab": pack_table(n((K, T)) * s1),
        "w4_words": p_w4[0],
        "w4_scales": p_w4[1],
        "x": (n((L, S)) * s2).astype(np.float32),
        "u": (n((L, M)) / np.sqrt(L) / s2).astype(np.float32),
        "r": (n((256, 256))).astype(np.float32),
        "offs": striped(np.random.permutation(T)[:S]),
    }


def reference(tab, w4_words, w4_scales, x, u, r, offs):
    tab_ = unpack_table(tab)[:, unstriped(offs)]
    w4_ = unpack_weight(w4_words, w4_scales, "e2m1")
    x_ = mxq(f64(x), 0, "e4m3")
    u_ = mxq(f64(u), 0, "e4m3")
    y = w4_.T @ tab_ + u_.T @ x_
    return f64(r) + y

@@ -1,0 +1,171 @@
+from contextlib import ExitStack
+
+import concourse.mybir as mybir
+
+K, L, M, T, S = 1536, 1536, 256, 512, 256
+P = 128
+PACK = 4
+PASSES = 3
+FLOPS = 2 * (K + L) * M * S
+
+F32 = mybir.dt.float32
+BF16 = mybir.dt.bfloat16
+I32 = mybir.dt.int32
+U32 = mybir.dt.uint32
+U16 = mybir.dt.uint16
+U8 = mybir.dt.uint8
+FP8X4 = mybir.dt.float8_e4m3fn_x4
+FP4X4 = mybir.dt.float4_e2m1fn_x4
+ADD = mybir.AluOpType.add
+
+
+def tile_list_tabx_res_kernel(tc, tab, w4_words, w4_scales, x, u, r, offs, out):
+    nc = tc.nc
+    with ExitStack() as ctx:
+        pool = ctx.enter_context(tc.tile_pool(name="keep", bufs=1))
+        psum = ctx.enter_context(tc.psum_pool(name="psum", bufs=1))
+
+        def sb(name, shape, dtype):
+            return pool.tile(shape, dtype, name=name, align_bytes=64)
+
+        offsets = pool.tile([P, S // 16], U16, name="offsets")
+        tw = [sb(f"tab_words{a}", [P, T], I32) for a in range(PASSES)]
+        ts = sb("tab_scales", [P, PASSES * T], U8)
+        ww = sb("w4_words_sb", [P, PASSES, 2 * M], U8)
+        ws = sb("w4_scales_sb", [P, PASSES * M], U8)
+        raw = {}
+        grouped = {}
+        codes = {}
+        scales = {}
+        for v in ("x", "u"):
+            for a in range(PASSES):
+                raw[v, a] = sb(f"{v}_raw{a}", [P, PACK, S], F32)
+                grouped[v, a] = sb(f"{v}_grouped{a}", [P, S, PACK], BF16)
+                codes[v, a] = sb(f"{v}_codes{a}", [P, S], U32)
+                scales[v, a] = sb(f"{v}_scales{a}", [P, S], U8)
+        gw = [sb(f"picked_words{a}", [P, S], U32) for a in range(PASSES)]
+        gs = [sb(f"picked_scales{a}", [P, S], U8) for a in range(PASSES)]
+        rs = sb("r_sb", [P, 2, S], F32)
+        res = [sb(f"result{m}", [P, S], F32) for m in range(2)]
+        acc = [psum.tile([P, S], F32, name=f"acc{m}") for m in range(2)]
+
+        nc.sync.dma_start(offsets[:], offs)
+
+        nc.vector.memset(ts[:].bitcast(I32), 0)
+        nc.vector.memset(ws[:].bitcast(I32), 0)
+
+        def load_tab(a):
+            nc.sync.dma_start(tw[a][:], tab[a, 0 : 4 * P * T].rearrange("(p b) -> p b", p=P).bitcast(I32))
+
+        hbm = {"x": x, "u": u}
+
+        def load_raw(v, a):
+            nc.sync.dma_start(
+                raw[v, a][:].rearrange("p j s -> p (j s)"),
+                hbm[v][4 * P * a : 4 * P * (a + 1), :].rearrange("(p j) s -> p (j s)", j=PACK),
+            )
+
+        tab_scale_rows = tab[:, 4 * P * T :].rearrange("a (q t) -> q a t", t=T)
+        for q in range(4):
+            nc.gpsimd.dma_start(
+                ts[32 * q : 32 * q + 4, :].rearrange("q (a t) -> q a t", a=PASSES).bitcast(I32),
+                tab_scale_rows[4 * q : 4 * q + 4, :, :].bitcast(I32),
+            )
+        w4_scale_rows = w4_scales.rearrange("a q n -> q a n")
+        for q in range(4):
+            nc.gpsimd.dma_start(
+                ws[32 * q : 32 * q + 4, :].rearrange("q (a n) -> q a n", a=PASSES).bitcast(I32),
+                w4_scale_rows[4 * q : 4 * q + 4, :, :].bitcast(I32),
+            )
+
+        load_tab(0)
+        load_raw("x", 0)
+        load_raw("u", 0)
+        load_tab(1)
+        load_raw("x", 1)
+        load_raw("u", 1)
+        nc.sync.dma_start(ww[:].bitcast(I32), w4_words.rearrange("a p b -> p a b").bitcast(I32))
+        load_tab(2)
+        load_raw("x", 2)
+        load_raw("u", 2)
+        for m in range(2):
+            nc.sync.dma_start(rs[:, m, :], r[P * m : P * (m + 1), :])
+
+        def interleave(engine, v, a, lo, hi):
+            dst = grouped[v, a][:, lo:hi, :].rearrange("p (c i) t -> p c t i", i=4)
+            src = raw[v, a][:, :, lo:hi].rearrange("p t (c i) -> p c t i", i=4)
+            if engine == "S":
+                nc.scalar.copy(dst, src)
+            else:
+                nc.vector.tensor_copy(dst, src)
+
+        def quantize(v, a):
+            nc.vector.quantize_mx(
+                out=codes[v, a][:].bitcast(FP8X4),
+                scales=scales[v, a][:],
+                in_=grouped[v, a][:].rearrange("p s t -> p (s t)"),
+            )
+
+        def pick_words(a):
+            nc.vector.tensor_copy(gw[a][:], tw[a][:].bitcast(U32).indirect(offsets[:]))
+
+        def pick_scales(a):
+            nc.vector.tensor_copy(gs[a][:], ts[:, T * a : T * (a + 1)].indirect(offsets[:]))
+
+        def own(a, start, stop):
+            for m in range(2):
+                cols = slice(P * m, P * (m + 1))
+                nc.tensor.matmul_mx(
+                    out=acc[m][:],
+                    lhsT=codes["u", a][:, cols].bitcast(FP8X4),
+                    lhsT_scale=scales["u", a][:, cols],
+                    rhs=codes["x", a][:].bitcast(FP8X4),
+                    rhs_scale=scales["x", a][:],
+                    start=start,
+                    stop=stop,
+                )
+
+        def memory(a):
+            for m in range(2):
+                for h in range(2):
+                    cols = slice(P * h, P * (h + 1))
+                    nc.tensor.matmul_mx(
+                        out=acc[m][:, cols],
+                        lhsT=ww[:, a, 2 * P * m : 2 * P * (m + 1)].bitcast(FP4X4),
+                        lhsT_scale=ws[:, M * a + P * m : M * a + P * (m + 1)],
+                        rhs=gw[a][:, cols].bitcast(FP8X4),
+                        rhs_scale=gs[a][:, cols],
+                        start=False,
+                        stop=False,
+                    )
+
+        pick_words(0)
+        interleave("S", "x", 0, 0, S)
+        interleave("S", "u", 0, 0, S)
+        quantize("x", 0)
+        pick_scales(0)
+        quantize("u", 0)
+        own(0, True, False)
+        pick_words(1)
+        pick_scales(1)
+        interleave("S", "x", 1, 0, S)
+        interleave("S", "u", 1, 0, S)
+        quantize("x", 1)
+        pick_words(2)
+        quantize("u", 1)
+        own(1, False, False)
+        memory(0)
+        memory(1)
+        interleave("S", "x", 2, 0, 128)
+        interleave("V", "x", 2, 128, S)
+        pick_scales(2)
+        quantize("x", 2)
+        memory(2)
+        interleave("S", "u", 2, 0, 96)
+        interleave("V", "u", 2, 96, S)
+        quantize("u", 2)
+        own(2, False, True)
+        for m in range(2):
+            nc.vector.tensor_tensor(res[m][:], acc[m][:], rs[:, m, :], ADD)
+            store = nc.sync if m == 0 else nc.scalar
+            store.dma_start(out[P * m : P * (m + 1), :], res[m][:])

@@ -33,139 +33,171 @@ def tile_list_tabx_res_kernel(tc, tab, w4_words, w4_scales, x, u, r, offs, out):
         ts = sb("tab_scales", [P, PASSES * T], U8)
         ww = sb("w4_words_sb", [P, PASSES, 2 * M], U8)
         ws = sb("w4_scales_sb", [P, PASSES * M], U8)
+        hbm = {"x": x, "u": u}
+        pieces = [("x", 0, 0, S), ("u", 0, 0, S), ("x", 1, 0, S), ("u", 1, 0, S), ("x", 2, 0, S), ("u", 2, 0, P), ("u", 2, P, S)]
         raw = {}
         grouped = {}
         codes = {}
         scales = {}
-        for v in ("x", "u"):
-            for a in range(PASSES):
-                raw[v, a] = sb(f"{v}_raw{a}", [P, PACK, S], F32)
-                grouped[v, a] = sb(f"{v}_grouped{a}", [P, S, PACK], BF16)
-                codes[v, a] = sb(f"{v}_codes{a}", [P, S], U32)
-                scales[v, a] = sb(f"{v}_scales{a}", [P, S], U8)
+        for v, a, lo, hi in pieces:
+            raw[v, a, lo] = sb(f"{v}_raw{a}_{lo}", [P, PACK, hi - lo], F32)
+            grouped[v, a, lo] = sb(f"{v}_grouped{a}_{lo}", [P, hi - lo, PACK], BF16)
+            codes[v, a, lo] = sb(f"{v}_codes{a}_{lo}", [P, hi - lo], U32)
+            scales[v, a, lo] = sb(f"{v}_scales{a}_{lo}", [P, hi - lo], U8)
         gw = [sb(f"picked_words{a}", [P, S], U32) for a in range(PASSES)]
         gs = [sb(f"picked_scales{a}", [P, S], U8) for a in range(PASSES)]
-        rs = sb("r_sb", [P, 2, S], F32)
+        rsb = sb("r_sb", [P, 2, S], F32)
+        rs = [rsb[:, m, :] for m in range(2)]
         res = [sb(f"result{m}", [P, S], F32) for m in range(2)]
-        acc = [psum.tile([P, S], F32, name=f"acc{m}") for m in range(2)]
+        acc = {(m, h): psum.tile([P, P], F32, name=f"acc{m}{h}") for m in range(2) for h in range(2)}
 
         nc.sync.dma_start(offsets[:], offs)
 
         nc.vector.memset(ts[:].bitcast(I32), 0)
         nc.vector.memset(ws[:].bitcast(I32), 0)
 
-        def load_tab(a):
-            nc.sync.dma_start(tw[a][:], tab[a, 0 : 4 * P * T].rearrange("(p b) -> p b", p=P).bitcast(I32))
+        def load_tab(a, q=nc.sync):
+            q.dma_start(tw[a][:], tab[a, 0 : 4 * P * T].rearrange("(p b) -> p b", p=P).bitcast(I32))
 
-        hbm = {"x": x, "u": u}
-
-        def load_raw(v, a):
-            nc.sync.dma_start(
-                raw[v, a][:].rearrange("p j s -> p (j s)"),
-                hbm[v][4 * P * a : 4 * P * (a + 1), :].rearrange("(p j) s -> p (j s)", j=PACK),
+        def load_raw(v, a, lo=0, hi=S, q=nc.sync):
+            q.dma_start(
+                raw[v, a, lo][:],
+                hbm[v][4 * P * a : 4 * P * (a + 1), lo:hi].rearrange("(p j) s -> p j s", j=PACK),
             )
 
-        tab_scale_rows = tab[:, 4 * P * T :].rearrange("a (q t) -> q a t", t=T)
-        for q in range(4):
-            nc.gpsimd.dma_start(
-                ts[32 * q : 32 * q + 4, :].rearrange("q (a t) -> q a t", a=PASSES).bitcast(I32),
-                tab_scale_rows[4 * q : 4 * q + 4, :, :].bitcast(I32),
-            )
-        w4_scale_rows = w4_scales.rearrange("a q n -> q a n")
-        for q in range(4):
-            nc.gpsimd.dma_start(
-                ws[32 * q : 32 * q + 4, :].rearrange("q (a n) -> q a n", a=PASSES).bitcast(I32),
-                w4_scale_rows[4 * q : 4 * q + 4, :, :].bitcast(I32),
-            )
+        tab_scale_rows = tab[:, 4 * P * T :].rearrange("a (quad row t) -> row quad a t", quad=4, row=4)
+        w4_scale_rows = w4_scales.rearrange("a (quad row) n -> row quad a n", row=4)
+
+        def load_tab_scales(queue):
+            for row in range(4):
+                queue.dma_start(
+                    ts[row : P : 32, :].rearrange("q (a t) -> q a t", a=PASSES).bitcast(I32),
+                    tab_scale_rows[row].bitcast(I32),
+                )
+
+        def load_w4_scales(queue):
+            for row in range(4):
+                queue.dma_start(
+                    ws[row : P : 32, :].rearrange("q (a n) -> q a n", a=PASSES).bitcast(I32),
+                    w4_scale_rows[row].bitcast(I32),
+                )
+
+        def load_w4(lo, hi, queue=nc.sync):
+            queue.dma_start(ww[:, lo:hi, :].bitcast(I32), w4_words[lo:hi].rearrange("a p b -> p a b").bitcast(I32))
+
+        def load_r(queue=nc.sync):
+            queue.dma_start(rsb[:], r.rearrange("(m p) j -> p m j", p=P))
 
         load_tab(0)
         load_raw("x", 0)
+        load_tab_scales(nc.sync)
         load_raw("u", 0)
         load_tab(1)
         load_raw("x", 1)
         load_raw("u", 1)
-        nc.sync.dma_start(ww[:].bitcast(I32), w4_words.rearrange("a p b -> p a b").bitcast(I32))
+        load_w4_scales(nc.sync)
+        load_w4(0, 2)
         load_tab(2)
         load_raw("x", 2)
-        load_raw("u", 2)
-        for m in range(2):
-            nc.sync.dma_start(rs[:, m, :], r[P * m : P * (m + 1), :])
+        load_raw("u", 2, 0, P)
+        load_raw("u", 2, P, S)
+        load_w4(2, 3)
+        load_r()
 
-        def interleave(engine, v, a, lo, hi):
-            dst = grouped[v, a][:, lo:hi, :].rearrange("p (c i) t -> p c t i", i=4)
-            src = raw[v, a][:, :, lo:hi].rearrange("p t (c i) -> p c t i", i=4)
+        def interleave(engine, v, a, base, lo, hi):
+            dst = grouped[v, a, base][:, lo:hi, :].rearrange("p (c i) t -> p c t i", i=4)
+            src = raw[v, a, base][:, :, lo:hi].rearrange("p t (c i) -> p c t i", i=4)
             if engine == "S":
                 nc.scalar.copy(dst, src)
             else:
                 nc.vector.tensor_copy(dst, src)
 
-        def quantize(v, a):
+        def quantize(v, a, base=0):
             nc.vector.quantize_mx(
-                out=codes[v, a][:].bitcast(FP8X4),
-                scales=scales[v, a][:],
-                in_=grouped[v, a][:].rearrange("p s t -> p (s t)"),
+                out=codes[v, a, base][:].bitcast(FP8X4),
+                scales=scales[v, a, base][:],
+                in_=grouped[v, a, base][:].rearrange("p s t -> p (s t)"),
             )
 
-        def pick_words(a):
-            nc.vector.tensor_copy(gw[a][:], tw[a][:].bitcast(U32).indirect(offsets[:]))
+        def pick_words(a, lo=0, hi=S):
+            nc.vector.tensor_copy(gw[a][:, lo:hi], tw[a][:].bitcast(U32).indirect(offsets[:, lo // 16 : hi // 16]))
 
         def pick_scales(a):
             nc.vector.tensor_copy(gs[a][:], ts[:, T * a : T * (a + 1)].indirect(offsets[:]))
 
-        def own(a, start, stop):
-            for m in range(2):
-                cols = slice(P * m, P * (m + 1))
-                nc.tensor.matmul_mx(
-                    out=acc[m][:],
-                    lhsT=codes["u", a][:, cols].bitcast(FP8X4),
-                    lhsT_scale=scales["u", a][:, cols],
-                    rhs=codes["x", a][:].bitcast(FP8X4),
-                    rhs_scale=scales["x", a][:],
-                    start=start,
-                    stop=stop,
-                )
+        def own(a, m, h, start, stop):
+            if ("u", a, P) in codes:
+                lc, ls = codes["u", a, P * m][:], scales["u", a, P * m][:]
+            else:
+                mc = slice(P * m, P * (m + 1))
+                lc, ls = codes["u", a, 0][:, mc], scales["u", a, 0][:, mc]
+            hc = slice(P * h, P * (h + 1))
+            nc.tensor.matmul_mx(
+                out=acc[m, h][:],
+                lhsT=lc.bitcast(FP8X4), lhsT_scale=ls,
+                rhs=codes["x", a, 0][:, hc].bitcast(FP8X4), rhs_scale=scales["x", a, 0][:, hc],
+                start=start, stop=stop,
+            )
 
-        def memory(a):
-            for m in range(2):
-                for h in range(2):
-                    cols = slice(P * h, P * (h + 1))
-                    nc.tensor.matmul_mx(
-                        out=acc[m][:, cols],
-                        lhsT=ww[:, a, 2 * P * m : 2 * P * (m + 1)].bitcast(FP4X4),
-                        lhsT_scale=ws[:, M * a + P * m : M * a + P * (m + 1)],
-                        rhs=gw[a][:, cols].bitcast(FP8X4),
-                        rhs_scale=gs[a][:, cols],
-                        start=False,
-                        stop=False,
-                    )
+        def memory(a, m, h, start, stop):
+            hc = slice(P * h, P * (h + 1))
+            nc.tensor.matmul_mx(
+                out=acc[m, h][:],
+                lhsT=ww[:, a, 2 * P * m : 2 * P * (m + 1)].bitcast(FP4X4),
+                lhsT_scale=ws[:, M * a + P * m : M * a + P * (m + 1)],
+                rhs=gw[a][:, hc].bitcast(FP8X4), rhs_scale=gs[a][:, hc],
+                start=start, stop=stop,
+            )
 
+        def add(m, h):
+            hc = slice(P * h, P * (h + 1))
+            nc.vector.tensor_tensor(res[m][:, hc], acc[m, h][:], rs[m][:, hc], ADD)
+
+        def store(m, queue):
+            queue.dma_start(out[P * m : P * (m + 1), :], res[m][:])
+
+        four = [(m, h) for m in range(2) for h in range(2)]
         pick_words(0)
-        interleave("S", "x", 0, 0, S)
-        interleave("S", "u", 0, 0, S)
-        quantize("x", 0)
+        interleave("S", "x", 0, 0, 0, S)
         pick_scales(0)
-        quantize("u", 0)
-        own(0, True, False)
-        pick_words(1)
         pick_scales(1)
-        interleave("S", "x", 1, 0, S)
-        interleave("S", "u", 1, 0, S)
-        quantize("x", 1)
-        pick_words(2)
-        quantize("u", 1)
-        own(1, False, False)
-        memory(0)
-        memory(1)
-        interleave("S", "x", 2, 0, 128)
-        interleave("V", "x", 2, 128, S)
         pick_scales(2)
+        quantize("x", 0)
+        interleave("S", "u", 0, 0, 0, S)
+        pick_words(1)
+        quantize("u", 0)
+        for m, h in four:
+            own(0, m, h, True, False)
+        interleave("S", "x", 1, 0, 0, 192)
+        interleave("V", "x", 1, 0, 192, S)
+        quantize("x", 1)
+        for m, h in four:
+            memory(0, m, h, False, False)
+        for m, h in four:
+            memory(1, m, h, False, False)
+        interleave("S", "u", 1, 0, 0, 192)
+        interleave("V", "u", 1, 0, 192, S)
+        quantize("u", 1)
+        for m, h in four:
+            own(1, m, h, False, False)
+        pick_words(2)
+        interleave("S", "x", 2, 0, 0, 96)
+        interleave("V", "x", 2, 0, 96, S)
+        for m, h in four:
+            memory(2, m, h, False, False)
+        interleave("S", "u", 2, 0, 0, P)
         quantize("x", 2)
-        memory(2)
-        interleave("S", "u", 2, 0, 96)
-        interleave("V", "u", 2, 96, S)
-        quantize("u", 2)
-        own(2, False, True)
-        for m in range(2):
-            nc.vector.tensor_tensor(res[m][:], acc[m][:], rs[:, m, :], ADD)
-            store = nc.sync if m == 0 else nc.scalar
-            store.dma_start(out[P * m : P * (m + 1), :], res[m][:])
+        interleave("S", "u", 2, P, 0, 40)
+        interleave("V", "u", 2, P, 40, P)
+        quantize("u", 2, 0)
+        own(2, 0, 0, False, True)
+        own(2, 0, 1, False, True)
+        quantize("u", 2, P)
+        own(2, 1, 0, False, True)
+        own(2, 1, 1, False, True)
+        add(0, 0)
+        add(0, 1)
+        store(0, nc.sync)
+        add(1, 0)
+        add(1, 1)
+        store(1, nc.sync)

from contextlib import ExitStack

import concourse.mybir as mybir

K, L, M, T, S = 1536, 1536, 256, 512, 256
P = 128
PACK = 4
PASSES = 3
FLOPS = 2 * (K + L) * M * S

F32 = mybir.dt.float32
BF16 = mybir.dt.bfloat16
I32 = mybir.dt.int32
U32 = mybir.dt.uint32
U16 = mybir.dt.uint16
U8 = mybir.dt.uint8
FP8X4 = mybir.dt.float8_e4m3fn_x4
FP4X4 = mybir.dt.float4_e2m1fn_x4
ADD = mybir.AluOpType.add


def tile_list_tabx_res_kernel(tc, tab, w4_words, w4_scales, x, u, r, offs, out):
    nc = tc.nc
    with ExitStack() as ctx:
        pool = ctx.enter_context(tc.tile_pool(name="keep", bufs=1))
        psum = ctx.enter_context(tc.psum_pool(name="psum", bufs=1))

        def sb(name, shape, dtype):
            return pool.tile(shape, dtype, name=name, align_bytes=64)

        offsets = pool.tile([P, S // 16], U16, name="offsets")
        tw = [sb(f"tab_words{a}", [P, T], I32) for a in range(PASSES)]
        ts = sb("tab_scales", [P, PASSES * T], U8)
        ww = sb("w4_words_sb", [P, PASSES, 2 * M], U8)
        ws = sb("w4_scales_sb", [P, PASSES * M], U8)
        hbm = {"x": x, "u": u}
        pieces = [("x", 0, 0, S), ("u", 0, 0, S), ("x", 1, 0, S), ("u", 1, 0, S), ("x", 2, 0, S), ("u", 2, 0, P), ("u", 2, P, S)]
        raw = {}
        grouped = {}
        codes = {}
        scales = {}
        for v, a, lo, hi in pieces:
            raw[v, a, lo] = sb(f"{v}_raw{a}_{lo}", [P, PACK, hi - lo], F32)
            grouped[v, a, lo] = sb(f"{v}_grouped{a}_{lo}", [P, hi - lo, PACK], BF16)
            codes[v, a, lo] = sb(f"{v}_codes{a}_{lo}", [P, hi - lo], U32)
            scales[v, a, lo] = sb(f"{v}_scales{a}_{lo}", [P, hi - lo], U8)
        gw = [sb(f"picked_words{a}", [P, S], U32) for a in range(PASSES)]
        gs = [sb(f"picked_scales{a}", [P, S], U8) for a in range(PASSES)]
        rsb = sb("r_sb", [P, 2, S], F32)
        rs = [rsb[:, m, :] for m in range(2)]
        res = [sb(f"result{m}", [P, S], F32) for m in range(2)]
        acc = {(m, h): psum.tile([P, P], F32, name=f"acc{m}{h}") for m in range(2) for h in range(2)}

        nc.sync.dma_start(offsets[:], offs)

        nc.vector.memset(ts[:].bitcast(I32), 0)
        nc.vector.memset(ws[:].bitcast(I32), 0)

        def load_tab(a, q=nc.sync):
            q.dma_start(tw[a][:], tab[a, 0 : 4 * P * T].rearrange("(p b) -> p b", p=P).bitcast(I32))

        def load_raw(v, a, lo=0, hi=S, q=nc.sync):
            q.dma_start(
                raw[v, a, lo][:],
                hbm[v][4 * P * a : 4 * P * (a + 1), lo:hi].rearrange("(p j) s -> p j s", j=PACK),
            )

        tab_scale_rows = tab[:, 4 * P * T :].rearrange("a (quad row t) -> row quad a t", quad=4, row=4)
        w4_scale_rows = w4_scales.rearrange("a (quad row) n -> row quad a n", row=4)

        def load_tab_scales(queue):
            for row in range(4):
                queue.dma_start(
                    ts[row : P : 32, :].rearrange("q (a t) -> q a t", a=PASSES).bitcast(I32),
                    tab_scale_rows[row].bitcast(I32),
                )

        def load_w4_scales(queue):
            for row in range(4):
                queue.dma_start(
                    ws[row : P : 32, :].rearrange("q (a n) -> q a n", a=PASSES).bitcast(I32),
                    w4_scale_rows[row].bitcast(I32),
                )

        def load_w4(lo, hi, queue=nc.sync):
            queue.dma_start(ww[:, lo:hi, :].bitcast(I32), w4_words[lo:hi].rearrange("a p b -> p a b").bitcast(I32))

        def load_r(queue=nc.sync):
            queue.dma_start(rsb[:], r.rearrange("(m p) j -> p m j", p=P))

        load_tab(0)
        load_raw("x", 0)
        load_tab_scales(nc.sync)
        load_raw("u", 0)
        load_tab(1)
        load_raw("x", 1)
        load_raw("u", 1)
        load_w4_scales(nc.sync)
        load_w4(0, 2)
        load_tab(2)
        load_raw("x", 2)
        load_raw("u", 2, 0, P)
        load_raw("u", 2, P, S)
        load_w4(2, 3)
        load_r()

        def interleave(engine, v, a, base, lo, hi):
            dst = grouped[v, a, base][:, lo:hi, :].rearrange("p (c i) t -> p c t i", i=4)
            src = raw[v, a, base][:, :, lo:hi].rearrange("p t (c i) -> p c t i", i=4)
            if engine == "S":
                nc.scalar.copy(dst, src)
            else:
                nc.vector.tensor_copy(dst, src)

        def quantize(v, a, base=0):
            nc.vector.quantize_mx(
                out=codes[v, a, base][:].bitcast(FP8X4),
                scales=scales[v, a, base][:],
                in_=grouped[v, a, base][:].rearrange("p s t -> p (s t)"),
            )

        def pick_words(a, lo=0, hi=S):
            nc.vector.tensor_copy(gw[a][:, lo:hi], tw[a][:].bitcast(U32).indirect(offsets[:, lo // 16 : hi // 16]))

        def pick_scales(a):
            nc.vector.tensor_copy(gs[a][:], ts[:, T * a : T * (a + 1)].indirect(offsets[:]))

        def own(a, m, h, start, stop):
            if ("u", a, P) in codes:
                lc, ls = codes["u", a, P * m][:], scales["u", a, P * m][:]
            else:
                mc = slice(P * m, P * (m + 1))
                lc, ls = codes["u", a, 0][:, mc], scales["u", a, 0][:, mc]
            hc = slice(P * h, P * (h + 1))
            nc.tensor.matmul_mx(
                out=acc[m, h][:],
                lhsT=lc.bitcast(FP8X4), lhsT_scale=ls,
                rhs=codes["x", a, 0][:, hc].bitcast(FP8X4), rhs_scale=scales["x", a, 0][:, hc],
                start=start, stop=stop,
            )

        def memory(a, m, h, start, stop):
            hc = slice(P * h, P * (h + 1))
            nc.tensor.matmul_mx(
                out=acc[m, h][:],
                lhsT=ww[:, a, 2 * P * m : 2 * P * (m + 1)].bitcast(FP4X4),
                lhsT_scale=ws[:, M * a + P * m : M * a + P * (m + 1)],
                rhs=gw[a][:, hc].bitcast(FP8X4), rhs_scale=gs[a][:, hc],
                start=start, stop=stop,
            )

        def add(m, h):
            hc = slice(P * h, P * (h + 1))
            nc.vector.tensor_tensor(res[m][:, hc], acc[m, h][:], rs[m][:, hc], ADD)

        def store(m, queue):
            queue.dma_start(out[P * m : P * (m + 1), :], res[m][:])

        four = [(m, h) for m in range(2) for h in range(2)]
        pick_words(0)
        interleave("S", "x", 0, 0, 0, S)
        pick_scales(0)
        pick_scales(1)
        pick_scales(2)
        quantize("x", 0)
        interleave("S", "u", 0, 0, 0, S)
        pick_words(1)
        quantize("u", 0)
        for m, h in four:
            own(0, m, h, True, False)
        interleave("S", "x", 1, 0, 0, 192)
        interleave("V", "x", 1, 0, 192, S)
        quantize("x", 1)
        for m, h in four:
            memory(0, m, h, False, False)
        for m, h in four:
            memory(1, m, h, False, False)
        interleave("S", "u", 1, 0, 0, 192)
        interleave("V", "u", 1, 0, 192, S)
        quantize("u", 1)
        for m, h in four:
            own(1, m, h, False, False)
        pick_words(2)
        interleave("S", "x", 2, 0, 0, 96)
        interleave("V", "x", 2, 0, 96, S)
        for m, h in four:
            memory(2, m, h, False, False)
        interleave("S", "u", 2, 0, 0, P)
        quantize("x", 2)
        interleave("S", "u", 2, P, 0, 40)
        interleave("V", "u", 2, P, 40, P)
        quantize("u", 2, 0)
        own(2, 0, 0, False, True)
        own(2, 0, 1, False, True)
        quantize("u", 2, P)
        own(2, 1, 0, False, True)
        own(2, 1, 1, False, True)
        add(0, 0)
        add(0, 1)
        store(0, nc.sync)
        add(1, 0)
        add(1, 1)
        store(1, nc.sync)
